import numpy as np
import ml_dtypes


def mxq(x, axis, fmt="e4m3"):
    dtype, down = {"e4m3": (ml_dtypes.float8_e4m3fn, 7), "e5m2": (ml_dtypes.float8_e5m2, 14)}[fmt]
    v = np.moveaxis(np.asarray(x, np.float32).astype(ml_dtypes.bfloat16).astype(np.float64), axis, -1)
    blocks = v.reshape(v.shape[:-1] + (-1, 32))
    amax = np.abs(blocks).max(-1, keepdims=True)
    byte = np.maximum(np.where(amax > 0, np.frexp(amax)[1] - 1 + 127, 0) - down, 1)
    scale = np.exp2(byte - 127.0)
    codes = (blocks / scale).astype(np.float32).astype(dtype).astype(np.float64)
    return np.moveaxis((codes * scale).reshape(v.shape), -1, axis)


WIDE = False


def mx_kscale(k):
    if not WIDE:
        return np.ones(k)
    levels = np.array([10, -10, 5, -5, 0])
    if k % 512:
        return np.exp2(np.random.permutation(np.resize(levels, k // 32))).repeat(32)
    a = np.empty((k // 512, 16))
    for p in range(k // 512):
        a[p, :8] = np.random.permutation(np.resize(levels, 8))
        for g in range(8):
            far = levels[np.abs(levels - a[p, g]) >= 10]
            a[p, g + 8] = far[np.random.randint(len(far))]
    return np.exp2(a.ravel()).repeat(32)


def f64(x):
    return np.asarray(x).astype(np.float64)


def striped(idx):
    return np.tile(idx.reshape(-1, 16).T, (8, 1)).astype(np.uint16)


def unstriped(offs):
    return offs[:16].T.reshape(-1).astype(np.int64)


def striped8(idx):
    return np.concatenate([x.reshape(-1, 16).T for x in idx]).astype(np.uint16)


def runs(offs, k):
    lists = np.stack([offs[16 * r : 16 * r + 16].T.reshape(-1) for r in range(8)]).astype(np.int64)
    return lists[np.arange(k) % 512 // 64]


def pack_weight(w):
    k, n = w.shape
    w = f64(np.asarray(w, np.float32).astype(ml_dtypes.bfloat16)).reshape(k // 32, 32, n)
    amax = np.abs(w).max(1)
    byte = np.clip(np.where(amax > 0, np.frexp(amax)[1] - 1 + 127 - 7, 1), 1, 254)
    scaled = (w * np.exp2(127.0 - byte)[:, None, :]).reshape(k, n).astype(np.float32)
    words = np.ascontiguousarray(scaled.reshape(k // 512, 128, 4, n).transpose(0, 1, 3, 2)).astype(ml_dtypes.float8_e4m3fn).view(np.uint8)
    return words, np.ascontiguousarray(byte.astype(np.uint8).reshape(k // 512, 16, n))


def unpack_weight(words, scales):
    g, p, n, _ = words.shape
    vals = np.ascontiguousarray(words).view(ml_dtypes.float8_e4m3fn).astype(np.float64) * np.repeat(np.exp2(scales.astype(np.float64) - 127.0), 8, axis=1)[..., None]
    return vals.transpose(0, 1, 3, 2).reshape(g * 512, n)


def sigmoid(v):
    return 1.0 / (1.0 + np.exp(-np.maximum(v, -700.0)))


K, T, S, H, C = 512, 2048, 512, 512, 512


def setup_inputs():
    n = np.random.standard_normal
    s = mx_kscale(K)[:, None]
    packed_xT = pack_weight(n((K, T)) * s)
    return {
        "x_words": packed_xT[0],
        "x_scales": packed_xT[1],
        "w1": (n((K, H)) / np.sqrt(K) / s).astype(np.float32),
        "w2": (n((K, H)) / np.sqrt(K) / s).astype(np.float32),
        "gs": (np.random.uniform(0.5, 1.5, (K, 1)) / s).astype(np.float32),
        "offs": striped(np.random.permutation(T)[:S]),
        "two": striped(np.random.permutation(T)[:S]),
        "n1": striped8(np.stack([np.random.permutation(S) for _ in range(8)])),
        "n2": striped8(np.stack([np.random.permutation(S) for _ in range(8)])),
        "cand": striped(np.random.permutation(T)[:C]),
        "n3": striped8(np.stack([np.random.permutation(S) for _ in range(8)])),
        "n4": striped8(np.stack([np.random.permutation(S) for _ in range(8)])),
    }


def reference(x_words, x_scales, w1, w2, gs, offs, two, n1, n2, cand, n3, n4):
    x_cand = unpack_weight(x_words, x_scales)[:, unstriped(cand)]
    xq = unpack_weight(x_words, x_scales)[:, unstriped(offs)]
    y = mxq(f64(w1), 0, "e4m3").T @ xq
    x_two = unpack_weight(x_words, x_scales)[:, unstriped(two)]
    d = mxq(f64(w2), 0, "e4m3").T @ x_two
    z = f64(gs) * (y + (sigmoid(d[np.arange(H)[:, None], runs(n2, H)] - d)) * (y[np.arange(H)[:, None], runs(n1, H)] - y))
    s = 0.0625 * ((x_cand.T @ mxq(z, 0, "e4m3")))
    st = s + s[np.arange(C)[:, None], runs(n3, C)]
    return st * (np.tanh(st[np.arange(C)[:, None], runs(n4, C)]))

@@ -1,0 +1,209 @@
+from contextlib import ExitStack
+
+import concourse.mybir as mybir
+
+K, T, S, H, C = 512, 2048, 512, 512, 512
+FLOPS = 2 * K * (2 * H * S + C * S)
+
+F32 = mybir.dt.float32
+BF16 = mybir.dt.bfloat16
+I32 = mybir.dt.int32
+U32 = mybir.dt.uint32
+U16 = mybir.dt.uint16
+U8 = mybir.dt.uint8
+FP8X4 = mybir.dt.float8_e4m3fn_x4
+ALU = mybir.AluOpType
+ACT = mybir.ActivationFunctionType
+
+P = 128
+PACK = 4
+W_HALF = H // 2
+Z_CHUNKS = ((0, 256), (256, 512))
+
+
+def tile_picked_twcpullbhopp_none_p_kernel(tc, x_words, x_scales, w1, w2, gs, offs, two, n1, n2, cand, n3, n4, out):
+    nc = tc.nc
+    with ExitStack() as ctx:
+        keep = ctx.enter_context(tc.tile_pool(name="keep", bufs=1))
+        psum = ctx.enter_context(tc.psum_pool(name="psum", bufs=1))
+
+        def sb(name, shape, dtype):
+            return keep.tile(shape, dtype, name=name, align_bytes=64)
+
+        def load_list(name, src):
+            tile = keep.tile([P, S // 16], U16, name=name)
+            nc.sync.dma_start(tile[:], src)
+            return tile
+
+        def load_weight_half(name, w, h):
+            tile = sb(name, [P, PACK, W_HALF], F32)
+            nc.sync.dma_start(tile[:], w.rearrange("(p j) c -> p j c", j=PACK)[:, :, h * W_HALF : (h + 1) * W_HALF])
+            return tile
+
+        table_scales = sb("table_scales", [P, T], U8)
+        table_words = sb("table_words", [P, T], U32)
+        d_win = [sb("d_win%d" % t, [P, 2 * S], F32) for t in range(PACK)]
+        y_win = [sb("y_win%d" % t, [P, 2 * S], F32) for t in range(PACK)]
+        s_win = [sb("s_win%d" % t, [P, 2 * S], F32) for t in range(PACK)]
+        st_win = [sb("st_win%d" % t, [P, 2 * S], F32) for t in range(PACK)]
+        d_last = sb("d_last", [P, S], F32)
+        s_last = sb("s_last", [P, S], F32)
+        d_twin = [d_win[t + 1][:, S:] for t in range(PACK - 1)] + [d_last[:]]
+        s_twin = [s_win[t + 1][:, S:] for t in range(PACK - 1)] + [s_last[:]]
+
+        nc.vector.memset(table_scales[:].bitcast(I32), 0)
+        two_l = load_list("two_l", two)
+        offs_l = load_list("offs_l", offs)
+        cand_l = load_list("cand_l", cand)
+        for q in range(4):
+            nc.sync.dma_start(table_scales[32 * q : 32 * q + 4, :].bitcast(I32), x_scales[0, 4 * q : 4 * q + 4, :].bitcast(I32))
+        w2_raw = [load_weight_half("w2_raw%d" % h, w2, h) for h in range(2)]
+        nc.sync.dma_start(table_words[:].bitcast(I32), x_words[0].rearrange("p c r -> p (c r)").bitcast(I32))
+        w1_raw = [load_weight_half("w1_raw%d" % h, w1, h) for h in range(2)]
+        n2_l = load_list("n2_l", n2)
+        gs_sb = sb("gs_sb", [P, PACK], F32)
+        nc.sync.dma_start(gs_sb[:], gs.rearrange("(p t) o -> p (t o)", t=PACK))
+        n1_l = load_list("n1_l", n1)
+        n3_l = load_list("n3_l", n3)
+        n4_l = load_list("n4_l", n4)
+
+        nc.vector.memset(d_win[0][:, S:], 0.0)
+        nc.scalar.activation(s_win[0][:, S:], d_win[0][:, S:], ACT.Sigmoid)
+
+        def gather_scales(name, lst):
+            tile = sb(name, [P, S], U8)
+            nc.vector.tensor_copy(tile[:], table_scales[:].indirect(lst[:]))
+            return tile
+
+        def gather_words(name, lst):
+            tile = sb(name, [P, S], U32)
+            nc.vector.tensor_copy(tile[:], table_words[:].indirect(lst[:]))
+            return tile
+
+        def round_weight(grouped, raw, h):
+            half_m = W_HALF // PACK
+            dst = grouped[:].rearrange("p (t m j) -> p m j t", t=PACK, j=PACK)[:, h * half_m : (h + 1) * half_m]
+            nc.scalar.copy(dst, raw[h][:].rearrange("p j (m t) -> p m j t", t=PACK))
+
+        def quantize(name, src, width):
+            codes = sb(name + "_codes", [P, width], U32)
+            scales = sb(name + "_scales", [P, width], U8)
+            nc.vector.quantize_mx(out=codes[:].bitcast(FP8X4), scales=scales[:], in_=src)
+            return codes, scales
+
+        def product(dst, lhs, t, rhs):
+            cols = slice(t * P, (t + 1) * P)
+            nc.tensor.matmul_mx(
+                out=dst, lhsT=lhs[0][:, cols].bitcast(FP8X4), lhsT_scale=lhs[1][:, cols],
+                rhs=rhs[0][:].bitcast(FP8X4), rhs_scale=rhs[1][:], start=True, stop=True,
+            )
+
+        w2_grouped = sb("w2_grouped", [P, PACK * H], BF16)
+        w1_grouped = sb("w1_grouped", [P, PACK * H], BF16)
+
+        two_scales = gather_scales("two_scales", two_l)
+        offs_scales = gather_scales("offs_scales", offs_l)
+        cand_scales_listed = gather_scales("cand_scales_listed", cand_l)
+        for h in range(2):
+            round_weight(w2_grouped, w2_raw, h)
+        w2_q = quantize("w2", w2_grouped[:], H)
+        two_words = gather_words("two_words", two_l)
+        d_ps = [psum.tile([P, S], F32, name="d_ps%d" % t, tag="bank%d" % t) for t in range(PACK)]
+        for t in range(PACK):
+            product(d_ps[t][:], w2_q, t, (two_words, two_scales))
+        offs_words = gather_words("offs_words", offs_l)
+        cand_words = sb("cand_words", [P, C], U32)
+        nc.vector.tensor_copy(cand_words[:].rearrange("p (t q u) -> p q t u", t=PACK, u=PACK), table_words[:].indirect(cand_l[:]))
+        cand_scales = sb("cand_scales", [P, C], U8)
+        nc.vector.tensor_copy(
+            cand_scales[:].bitcast(I32).rearrange("p (t q) -> p t q", t=PACK),
+            cand_scales_listed[:].bitcast(I32).rearrange("p (q t) -> p t q", t=PACK),
+        )
+
+        def d_out(t):
+            nc.scalar.copy(d_win[t][:, :S], d_ps[t][:])
+            nc.scalar.copy(d_twin[t], d_ps[t][:])
+
+        def d_diff(t):
+            nc.vector.tensor_tensor(y_win[t][:, S:], d_win[t][:].indirect(n2_l[:]), d_twin[t], ALU.subtract)
+
+        round_weight(w1_grouped, w1_raw, 0)
+        d_out(0)
+        round_weight(w1_grouped, w1_raw, 1)
+        d_out(1)
+        d_diff(0)
+        w1_q = quantize("w1", w1_grouped[:], H)
+        d_diff(1)
+        y_ps = [psum.tile([P, S], F32, name="y_ps%d" % t, tag="bank%d" % (PACK + t)) for t in range(PACK)]
+        for t in range(PACK):
+            product(y_ps[t][:], w1_q, t, (offs_words, offs_scales))
+        for t in range(2, PACK):
+            d_out(t)
+            d_diff(t)
+
+        pulled = sb("pulled", [P, PACK, S], F32)
+        stayed = sb("stayed", [P, PACK, S], F32)
+
+        def pull(t, lo, hi):
+            nc.vector.tensor_tensor(pulled[:, t, lo:hi], y_win[t][:].indirect(n1_l[:, lo // 16 : hi // 16]), st_win[t][:, S + lo : S + hi], ALU.mult)
+
+        def scores(c):
+            lo, hi = Z_CHUNKS[c]
+            width = hi - lo
+            z_grouped = sb("z_grouped%d" % c, [P, PACK * width], BF16)
+            nc.vector.tensor_tensor(
+                z_grouped[:].rearrange("p (c i t) -> p c t i", i=PACK, t=PACK),
+                pulled[:, :, lo:hi].rearrange("p t (c i) -> p c t i", i=PACK),
+                stayed[:, :, lo:hi].rearrange("p t (c i) -> p c t i", i=PACK),
+                ALU.subtract,
+            )
+            z_q = quantize("z%d" % c, z_grouped[:], width)
+            banks = [psum.tile([P, width], F32, name="s_ps%d_%d" % (c, t), tag="bank%d" % (PACK * c + t)) for t in range(PACK)]
+            for t in range(PACK):
+                product(banks[t][:], (cand_words, cand_scales), t, z_q)
+            return banks
+
+        def s_out(c, t, banks):
+            lo, hi = Z_CHUNKS[c]
+            nc.scalar.activation(s_win[t][:, lo:hi], banks[t][:], ACT.Copy, scale=0.125)
+            nc.scalar.activation(s_twin[t][:, lo:hi], banks[t][:], ACT.Copy, scale=0.125)
+
+        for t in range(PACK):
+            gate = st_win[t][:, S:]
+            nc.scalar.activation(gate, y_win[t][:, S:], ACT.Sigmoid)
+            nc.scalar.activation(y_win[t][:, :S], y_ps[t][:], ACT.Copy, scale=gs_sb[:, t : t + 1])
+            nc.vector.scalar_tensor_tensor(stayed[:, t, :], gate, 1.0, y_win[t][:, :S], ALU.subtract, ALU.mult)
+            pull(t, *Z_CHUNKS[0])
+        first = scores(0)
+        for t in range(PACK):
+            s_out(0, t, first)
+            pull(t, *Z_CHUNKS[1])
+        second = scores(1)
+
+        rows = out.rearrange("(q t u) n -> t q u n", t=PACK, u=PACK)
+        squash = [sb("squash%d" % t, [P, S], F32) for t in range(PACK)]
+        result = [sb("result%d" % t, [P, S], F32) for t in range(PACK)]
+
+        def pair_up(t):
+            nc.vector.tensor_tensor(st_win[t][:, :S], s_win[t][:].indirect(n3_l[:]), s_twin[t], ALU.add)
+
+        def look_up(t, lo, hi):
+            nc.scalar.activation(squash[t][:, lo:hi], st_win[t][:].indirect(n4_l[:, lo // 16 : hi // 16]), ACT.Sigmoid)
+
+        def finish(t, lo, hi):
+            nc.vector.scalar_tensor_tensor(result[t][:, lo:hi], squash[t][:, lo:hi], 0.5, st_win[t][:, lo:hi], ALU.subtract, ALU.mult)
+            nc.sync.dma_start(rows[t][:, :, lo:hi], result[t][:, lo:hi])
+
+        for t in range(PACK - 1):
+            s_out(1, t, second)
+            pair_up(t)
+        look_up(0, 0, S)
+        finish(0, 0, S)
+        s_out(1, PACK - 1, second)
+        pair_up(PACK - 1)
+        for t in range(1, PACK - 1):
+            look_up(t, 0, S)
+            finish(t, 0, S)
+        for lo in (0, S // 2):
+            look_up(PACK - 1, lo, lo + S // 2)
+            finish(PACK - 1, lo, lo + S // 2)

@@ -18,7 +18,6 @@ ACT = mybir.ActivationFunctionType
 P = 128
 PACK = 4
 W_HALF = H // 2
-Z_CHUNKS = ((0, 256), (256, 512))
 
 
 def tile_picked_twcpullbhopp_none_p_kernel(tc, x_words, x_scales, w1, w2, gs, offs, two, n1, n2, cand, n3, n4, out):
@@ -46,10 +45,12 @@ def tile_picked_twcpullbhopp_none_p_kernel(tc, x_words, x_scales, w1, w2, gs, of
         y_win = [sb("y_win%d" % t, [P, 2 * S], F32) for t in range(PACK)]
         s_win = [sb("s_win%d" % t, [P, 2 * S], F32) for t in range(PACK)]
         st_win = [sb("st_win%d" % t, [P, 2 * S], F32) for t in range(PACK)]
-        d_last = sb("d_last", [P, S], F32)
         s_last = sb("s_last", [P, S], F32)
-        d_twin = [d_win[t + 1][:, S:] for t in range(PACK - 1)] + [d_last[:]]
+        d_twin = [d_win[t + 1][:, S:] for t in range(PACK - 1)] + [y_win[PACK - 1][:, S:]]
         s_twin = [s_win[t + 1][:, S:] for t in range(PACK - 1)] + [s_last[:]]
+
+        last_diff = keep.tile([P, S], F32, name="last_diff", tag="late", align_bytes=64)
+        diff = [y_win[t][:, S:] for t in range(PACK - 1)] + [last_diff[:]]
 
         nc.vector.memset(table_scales[:].bitcast(I32), 0)
         two_l = load_list("two_l", two)
@@ -125,7 +126,7 @@ def tile_picked_twcpullbhopp_none_p_kernel(tc, x_words, x_scales, w1, w2, gs, of
             nc.scalar.copy(d_twin[t], d_ps[t][:])
 
         def d_diff(t):
-            nc.vector.tensor_tensor(y_win[t][:, S:], d_win[t][:].indirect(n2_l[:]), d_twin[t], ALU.subtract)
+            nc.vector.tensor_tensor(diff[t], d_win[t][:].indirect(n2_l[:]), d_twin[t], ALU.subtract)
 
         round_weight(w1_grouped, w1_raw, 0)
         d_out(0)
@@ -141,51 +142,69 @@ def tile_picked_twcpullbhopp_none_p_kernel(tc, x_words, x_scales, w1, w2, gs, of
             d_out(t)
             d_diff(t)
 
-        pulled = sb("pulled", [P, PACK, S], F32)
+        HALF = S // 2
+        QUARTER = S // 4
         stayed = sb("stayed", [P, PACK, S], F32)
+        pulled_early = sb("pulled_early", [P, PACK, HALF], F32)
 
-        def pull(t, lo, hi):
-            nc.vector.tensor_tensor(pulled[:, t, lo:hi], y_win[t][:].indirect(n1_l[:, lo // 16 : hi // 16]), st_win[t][:, S + lo : S + hi], ALU.mult)
+        def pull(dst, t, lo, hi):
+            nc.vector.tensor_tensor(dst, y_win[t][:].indirect(n1_l[:, lo // 16 : hi // 16]), st_win[t][:, S + lo : S + hi], ALU.mult)
 
-        def scores(c):
-            lo, hi = Z_CHUNKS[c]
-            width = hi - lo
-            z_grouped = sb("z_grouped%d" % c, [P, PACK * width], BF16)
+        def blend(z_grouped, pulled, lo, hi):
             nc.vector.tensor_tensor(
-                z_grouped[:].rearrange("p (c i t) -> p c t i", i=PACK, t=PACK),
-                pulled[:, :, lo:hi].rearrange("p t (c i) -> p c t i", i=PACK),
+                z_grouped.rearrange("p (c i t) -> p c t i", i=PACK, t=PACK),
+                pulled.rearrange("p t (c i) -> p c t i", i=PACK),
                 stayed[:, :, lo:hi].rearrange("p t (c i) -> p c t i", i=PACK),
                 ALU.subtract,
             )
-            z_q = quantize("z%d" % c, z_grouped[:], width)
-            banks = [psum.tile([P, width], F32, name="s_ps%d_%d" % (c, t), tag="bank%d" % (PACK * c + t)) for t in range(PACK)]
-            for t in range(PACK):
-                product(banks[t][:], (cand_words, cand_scales), t, z_q)
-            return banks
 
-        def s_out(c, t, banks):
-            lo, hi = Z_CHUNKS[c]
-            nc.scalar.activation(s_win[t][:, lo:hi], banks[t][:], ACT.Copy, scale=0.125)
-            nc.scalar.activation(s_twin[t][:, lo:hi], banks[t][:], ACT.Copy, scale=0.125)
+        def s_out(t, lo, hi, bank):
+            nc.scalar.activation(s_win[t][:, lo:hi], bank, ACT.Copy, scale=0.125)
+            nc.scalar.activation(s_twin[t][:, lo:hi], bank, ACT.Copy, scale=0.125)
 
+        cand_q = (cand_words, cand_scales)
         for t in range(PACK):
             gate = st_win[t][:, S:]
-            nc.scalar.activation(gate, y_win[t][:, S:], ACT.Sigmoid)
             nc.scalar.activation(y_win[t][:, :S], y_ps[t][:], ACT.Copy, scale=gs_sb[:, t : t + 1])
+            nc.scalar.activation(gate, diff[t], ACT.Sigmoid)
             nc.vector.scalar_tensor_tensor(stayed[:, t, :], gate, 1.0, y_win[t][:, :S], ALU.subtract, ALU.mult)
-            pull(t, *Z_CHUNKS[0])
-        first = scores(0)
+            pull(pulled_early[:, t, :], t, 0, HALF)
+
+        pulled_late = keep.tile([P, PACK, HALF], F32, name="pulled_late", tag="late", align_bytes=64)
+        z_early = sb("z_early", [P, PACK * HALF], BF16)
+        pull(pulled_late[:, 0, :], 0, HALF, S)
+        blend(z_early[:], pulled_early[:], 0, HALF)
+        pull(pulled_late[:, 1, :], 1, HALF, S)
+        z_early_q = quantize("z_early", z_early[:], HALF)
         for t in range(PACK):
-            s_out(0, t, first)
-            pull(t, *Z_CHUNKS[1])
-        second = scores(1)
+            bank = psum.tile([P, HALF], F32, name="s_early%d" % t, tag="bank%d" % t)
+            product(bank[:], cand_q, t, z_early_q)
+            s_out(t, 0, HALF, bank[:])
+        pull(pulled_late[:, 2, :], 2, HALF, S)
+        for lo in (0, QUARTER):
+            pull(pulled_late[:, 3, lo : lo + QUARTER], 3, HALF + lo, HALF + lo + QUARTER)
+        z_late = sb("z_late", [P, PACK * HALF], BF16)
+        z_late_codes = sb("z_late_codes", [P, HALF], U32)
+        z_late_scales = sb("z_late_scales", [P, HALF], U8)
+        for lo in (0, QUARTER):
+            blend(z_late[:, PACK * lo : PACK * (lo + QUARTER)], pulled_late[:, :, lo : lo + QUARTER], HALF + lo, HALF + lo + QUARTER)
+        for i, lo in enumerate((0, QUARTER)):
+            cols = slice(lo, lo + QUARTER)
+            nc.vector.quantize_mx(out=z_late_codes[:, cols].bitcast(FP8X4), scales=z_late_scales[:, cols], in_=z_late[:, PACK * lo : PACK * (lo + QUARTER)])
+            bank = psum.tile([P, QUARTER], F32, name="s_first%d" % i, tag="bank%d" % (PACK * i))
+            product(bank[:], cand_q, 0, (z_late_codes[:, cols], z_late_scales[:, cols]))
+            s_out(0, HALF + lo, HALF + lo + QUARTER, bank[:])
+        late = {}
+        for t in range(1, PACK):
+            late[t] = psum.tile([P, HALF], F32, name="s_late%d" % t, tag="bank%d" % (PACK + t))
+            product(late[t][:], cand_q, t, (z_late_codes, z_late_scales))
 
         rows = out.rearrange("(q t u) n -> t q u n", t=PACK, u=PACK)
         squash = [sb("squash%d" % t, [P, S], F32) for t in range(PACK)]
         result = [sb("result%d" % t, [P, S], F32) for t in range(PACK)]
 
-        def pair_up(t):
-            nc.vector.tensor_tensor(st_win[t][:, :S], s_win[t][:].indirect(n3_l[:]), s_twin[t], ALU.add)
+        def pair_up(t, lo=0, hi=S):
+            nc.vector.tensor_tensor(st_win[t][:, lo:hi], s_win[t][:].indirect(n3_l[:, lo // 16 : hi // 16]), s_twin[t][:, lo:hi], ALU.add)
 
         def look_up(t, lo, hi):
             nc.scalar.activation(squash[t][:, lo:hi], st_win[t][:].indirect(n4_l[:, lo // 16 : hi // 16]), ACT.Sigmoid)
@@ -194,12 +213,14 @@ def tile_picked_twcpullbhopp_none_p_kernel(tc, x_words, x_scales, w1, w2, gs, of
             nc.vector.scalar_tensor_tensor(result[t][:, lo:hi], squash[t][:, lo:hi], 0.5, st_win[t][:, lo:hi], ALU.subtract, ALU.mult)
             nc.sync.dma_start(rows[t][:, :, lo:hi], result[t][:, lo:hi])
 
-        for t in range(PACK - 1):
-            s_out(1, t, second)
+        pair_up(0, 0, HALF)
+        pair_up(0, HALF, S)
+        for t in range(1, PACK - 1):
+            s_out(t, HALF, S, late[t][:])
             pair_up(t)
         look_up(0, 0, S)
         finish(0, 0, S)
-        s_out(1, PACK - 1, second)
+        s_out(PACK - 1, HALF, S, late[PACK - 1][:])
         pair_up(PACK - 1)
         for t in range(1, PACK - 1):
             look_up(t, 0, S)

@@ -18,6 +18,7 @@ ACT = mybir.ActivationFunctionType
 P = 128
 PACK = 4
 W_HALF = H // 2
+X_HEAD = 512
 
 
 def tile_picked_twcpullbhopp_none_p_kernel(tc, x_words, x_scales, w1, w2, gs, offs, two, n1, n2, cand, n3, n4, out):
@@ -53,13 +54,16 @@ def tile_picked_twcpullbhopp_none_p_kernel(tc, x_words, x_scales, w1, w2, gs, of
         diff = [y_win[t][:, S:] for t in range(PACK - 1)] + [last_diff[:]]
 
         nc.vector.memset(table_scales[:].bitcast(I32), 0)
+        words_in_hbm = x_words[0].rearrange("p c r -> p (c r)").bitcast(I32)
+        nc.sync.dma_start(table_words[:, :X_HEAD].bitcast(I32), words_in_hbm[:, :X_HEAD])
         two_l = load_list("two_l", two)
         offs_l = load_list("offs_l", offs)
+        for r in range(4):
+            nc.sync.dma_start(table_scales[r:P:32, :].bitcast(I32), x_scales[0, r:16:4, :].bitcast(I32))
+        w2_raw = [load_weight_half("w2_raw0", w2, 0)]
         cand_l = load_list("cand_l", cand)
-        for q in range(4):
-            nc.sync.dma_start(table_scales[32 * q : 32 * q + 4, :].bitcast(I32), x_scales[0, 4 * q : 4 * q + 4, :].bitcast(I32))
-        w2_raw = [load_weight_half("w2_raw%d" % h, w2, h) for h in range(2)]
-        nc.sync.dma_start(table_words[:].bitcast(I32), x_words[0].rearrange("p c r -> p (c r)").bitcast(I32))
+        w2_raw.append(load_weight_half("w2_raw1", w2, 1))
+        nc.sync.dma_start(table_words[:, X_HEAD:].bitcast(I32), words_in_hbm[:, X_HEAD:])
         w1_raw = [load_weight_half("w1_raw%d" % h, w1, h) for h in range(2)]
         n2_l = load_list("n2_l", n2)
         gs_sb = sb("gs_sb", [P, PACK], F32)
@@ -215,14 +219,10 @@ def tile_picked_twcpullbhopp_none_p_kernel(tc, x_words, x_scales, w1, w2, gs, of
 
         pair_up(0, 0, HALF)
         pair_up(0, HALF, S)
-        for t in range(1, PACK - 1):
+        for t in range(1, PACK):
             s_out(t, HALF, S, late[t][:])
             pair_up(t)
-        look_up(0, 0, S)
-        finish(0, 0, S)
-        s_out(PACK - 1, HALF, S, late[PACK - 1][:])
-        pair_up(PACK - 1)
-        for t in range(1, PACK - 1):
+        for t in range(PACK - 1):
             look_up(t, 0, S)
             finish(t, 0, S)
         for lo in (0, S // 2):

@@ -17,8 +17,6 @@ ACT = mybir.ActivationFunctionType
 
 P = 128
 PACK = 4
-W_HALF = H // 2
-X_HEAD = 512
 
 
 def tile_picked_twcpullbhopp_none_p_kernel(tc, x_words, x_scales, w1, w2, gs, offs, two, n1, n2, cand, n3, n4, out):
@@ -35,10 +33,10 @@ def tile_picked_twcpullbhopp_none_p_kernel(tc, x_words, x_scales, w1, w2, gs, of
             nc.sync.dma_start(tile[:], src)
             return tile
 
-        def load_weight_half(name, w, h):
-            tile = sb(name, [P, PACK, W_HALF], F32)
-            nc.sync.dma_start(tile[:], w.rearrange("(p j) c -> p j c", j=PACK)[:, :, h * W_HALF : (h + 1) * W_HALF])
-            return tile
+        def load_weight(name, w, lo, hi):
+            tile = sb("%s_raw%d" % (name, lo), [P, PACK, hi - lo], F32)
+            nc.sync.dma_start(tile[:], w.rearrange("(p j) c -> p j c", j=PACK)[:, :, lo:hi])
+            return tile, lo, hi
 
         table_scales = sb("table_scales", [P, T], U8)
         table_words = sb("table_words", [P, T], U32)
@@ -54,17 +52,16 @@ def tile_picked_twcpullbhopp_none_p_kernel(tc, x_words, x_scales, w1, w2, gs, of
         diff = [y_win[t][:, S:] for t in range(PACK - 1)] + [last_diff[:]]
 
         nc.vector.memset(table_scales[:].bitcast(I32), 0)
-        words_in_hbm = x_words[0].rearrange("p c r -> p (c r)").bitcast(I32)
-        nc.sync.dma_start(table_words[:, :X_HEAD].bitcast(I32), words_in_hbm[:, :X_HEAD])
+        w2_raw = [load_weight("w2", w2, 0, 128)]
         two_l = load_list("two_l", two)
         offs_l = load_list("offs_l", offs)
         for r in range(4):
             nc.sync.dma_start(table_scales[r:P:32, :].bitcast(I32), x_scales[0, r:16:4, :].bitcast(I32))
-        w2_raw = [load_weight_half("w2_raw0", w2, 0)]
+        w2_raw.append(load_weight("w2", w2, 128, 384))
         cand_l = load_list("cand_l", cand)
-        w2_raw.append(load_weight_half("w2_raw1", w2, 1))
-        nc.sync.dma_start(table_words[:, X_HEAD:].bitcast(I32), words_in_hbm[:, X_HEAD:])
-        w1_raw = [load_weight_half("w1_raw%d" % h, w1, h) for h in range(2)]
+        w2_raw.append(load_weight("w2", w2, 384, 512))
+        nc.sync.dma_start(table_words[:].bitcast(I32), x_words[0].rearrange("p c r -> p (c r)").bitcast(I32))
+        w1_raw = [load_weight("w1", w1, lo, hi) for lo, hi in ((0, 128), (128, 256), (256, 512))]
         n2_l = load_list("n2_l", n2)
         gs_sb = sb("gs_sb", [P, PACK], F32)
         nc.sync.dma_start(gs_sb[:], gs.rearrange("(p t) o -> p (t o)", t=PACK))
@@ -85,10 +82,10 @@ def tile_picked_twcpullbhopp_none_p_kernel(tc, x_words, x_scales, w1, w2, gs, of
             nc.vector.tensor_copy(tile[:], table_words[:].indirect(lst[:]))
             return tile
 
-        def round_weight(grouped, raw, h):
-            half_m = W_HALF // PACK
-            dst = grouped[:].rearrange("p (t m j) -> p m j t", t=PACK, j=PACK)[:, h * half_m : (h + 1) * half_m]
-            nc.scalar.copy(dst, raw[h][:].rearrange("p j (m t) -> p m j t", t=PACK))
+        def round_weight(grouped, piece):
+            raw, lo, hi = piece
+            dst = grouped[:].rearrange("p (t m j) -> p m j t", t=PACK, j=PACK)[:, lo // PACK : hi // PACK]
+            nc.scalar.copy(dst, raw[:].rearrange("p j (m t) -> p m j t", t=PACK))
 
         def quantize(name, src, width):
             codes = sb(name + "_codes", [P, width], U32)
@@ -109,8 +106,8 @@ def tile_picked_twcpullbhopp_none_p_kernel(tc, x_words, x_scales, w1, w2, gs, of
         two_scales = gather_scales("two_scales", two_l)
         offs_scales = gather_scales("offs_scales", offs_l)
         cand_scales_listed = gather_scales("cand_scales_listed", cand_l)
-        for h in range(2):
-            round_weight(w2_grouped, w2_raw, h)
+        for piece in w2_raw:
+            round_weight(w2_grouped, piece)
         w2_q = quantize("w2", w2_grouped[:], H)
         two_words = gather_words("two_words", two_l)
         d_ps = [psum.tile([P, S], F32, name="d_ps%d" % t, tag="bank%d" % t) for t in range(PACK)]
@@ -132,9 +129,10 @@ def tile_picked_twcpullbhopp_none_p_kernel(tc, x_words, x_scales, w1, w2, gs, of
         def d_diff(t):
             nc.vector.tensor_tensor(diff[t], d_win[t][:].indirect(n2_l[:]), d_twin[t], ALU.subtract)
 
-        round_weight(w1_grouped, w1_raw, 0)
+        round_weight(w1_grouped, w1_raw[0])
+        round_weight(w1_grouped, w1_raw[1])
         d_out(0)
-        round_weight(w1_grouped, w1_raw, 1)
+        round_weight(w1_grouped, w1_raw[2])
         d_out(1)
         d_diff(0)
         w1_q = quantize("w1", w1_grouped[:], H)
@@ -197,7 +195,11 @@ def tile_picked_twcpullbhopp_none_p_kernel(tc, x_words, x_scales, w1, w2, gs, of
             nc.vector.quantize_mx(out=z_late_codes[:, cols].bitcast(FP8X4), scales=z_late_scales[:, cols], in_=z_late[:, PACK * lo : PACK * (lo + QUARTER)])
             bank = psum.tile([P, QUARTER], F32, name="s_first%d" % i, tag="bank%d" % (PACK * i))
             product(bank[:], cand_q, 0, (z_late_codes[:, cols], z_late_scales[:, cols]))
-            s_out(0, HALF + lo, HALF + lo + QUARTER, bank[:])
+            if i == 0:
+                s_out(0, HALF + lo, HALF + lo + QUARTER, bank[:])
+            else:
+                nc.vector.tensor_scalar(s_win[0][:, HALF + lo : S], bank[:], 0.125, None, ALU.mult)
+                nc.scalar.activation(s_twin[0][:, HALF + lo : S], bank[:], ACT.Copy, scale=0.125)
         late = {}
         for t in range(1, PACK):
             late[t] = psum.tile([P, HALF], F32, name="s_late%d" % t, tag="bank%d" % (PACK + t))
@@ -225,6 +227,6 @@ def tile_picked_twcpullbhopp_none_p_kernel(tc, x_words, x_scales, w1, w2, gs, of
         for t in range(PACK - 1):
             look_up(t, 0, S)
             finish(t, 0, S)
-        for lo in (0, S // 2):
-            look_up(PACK - 1, lo, lo + S // 2)
-            finish(PACK - 1, lo, lo + S // 2)
+        for lo, hi in ((0, HALF), (HALF, S)):
+            look_up(PACK - 1, lo, hi)
+            finish(PACK - 1, lo, hi)

@@ -17,9 +17,22 @@ ACT = mybir.ActivationFunctionType
 
 P = 128
 PACK = 4
+LAST = PACK - 1
+STRIPE = 16
+QUADRANT = 32
+SCALE_ROWS = 4
+HALF = S // 2
+QUARTER = S // 4
+S_SCALE = 2 * 0.0625
+PAIR = 2
+
+W2_PIECES = ((0, 128), (128, 384), (384, 512))
+W1_PIECES = ((0, 128), (128, 256), (256, 512))
 
 
-def tile_picked_twcpullbhopp_none_p_kernel(tc, x_words, x_scales, w1, w2, gs, offs, two, n1, n2, cand, n3, n4, out):
+def tile_picked_twcpullbhopp_none_p_kernel(
+    tc, x_words, x_scales, w1, w2, gs, offs, two, n1, n2, cand, n3, n4, out
+):
     nc = tc.nc
     with ExitStack() as ctx:
         keep = ctx.enter_context(tc.tile_pool(name="keep", bufs=1))
@@ -28,10 +41,16 @@ def tile_picked_twcpullbhopp_none_p_kernel(tc, x_words, x_scales, w1, w2, gs, of
         def sb(name, shape, dtype):
             return keep.tile(shape, dtype, name=name, align_bytes=64)
 
+        def bank_tile(name, width, bank_no):
+            return psum.tile([P, width], F32, name=name, tag="bank%d" % bank_no)
+
         def load_list(name, src):
-            tile = keep.tile([P, S // 16], U16, name=name)
+            tile = keep.tile([P, S // STRIPE], U16, name=name)
             nc.sync.dma_start(tile[:], src)
             return tile
+
+        def entries(lst, lo, hi):
+            return lst[:, lo // STRIPE : hi // STRIPE]
 
         def load_weight(name, w, lo, hi):
             tile = sb("%s_raw%d" % (name, lo), [P, PACK, hi - lo], F32)
@@ -45,23 +64,23 @@ def tile_picked_twcpullbhopp_none_p_kernel(tc, x_words, x_scales, w1, w2, gs, of
         s_win = [sb("s_win%d" % t, [P, 2 * S], F32) for t in range(PACK)]
         st_win = [sb("st_win%d" % t, [P, 2 * S], F32) for t in range(PACK)]
         s_last = sb("s_last", [P, S], F32)
-        d_twin = [d_win[t + 1][:, S:] for t in range(PACK - 1)] + [y_win[PACK - 1][:, S:]]
-        s_twin = [s_win[t + 1][:, S:] for t in range(PACK - 1)] + [s_last[:]]
-
         last_diff = keep.tile([P, S], F32, name="last_diff", tag="late", align_bytes=64)
-        diff = [y_win[t][:, S:] for t in range(PACK - 1)] + [last_diff[:]]
+        d_twin = [d_win[t + 1][:, S:] for t in range(LAST)] + [y_win[LAST][:, S:]]
+        s_twin = [s_win[t + 1][:, S:] for t in range(LAST)] + [s_last[:]]
+        diff = [y_win[t][:, S:] for t in range(LAST)] + [last_diff[:]]
+        gate = [st_win[t][:, S:] for t in range(PACK)]
 
         nc.vector.memset(table_scales[:].bitcast(I32), 0)
-        w2_raw = [load_weight("w2", w2, 0, 128)]
+        w2_raw = [load_weight("w2", w2, *W2_PIECES[0])]
         two_l = load_list("two_l", two)
         offs_l = load_list("offs_l", offs)
-        for r in range(4):
-            nc.sync.dma_start(table_scales[r:P:32, :].bitcast(I32), x_scales[0, r:16:4, :].bitcast(I32))
-        w2_raw.append(load_weight("w2", w2, 128, 384))
+        for r in range(SCALE_ROWS):
+            nc.sync.dma_start(table_scales[r:P:QUADRANT, :].bitcast(I32), x_scales[0, r : K // 32 : SCALE_ROWS, :].bitcast(I32))
+        w2_raw.append(load_weight("w2", w2, *W2_PIECES[1]))
         cand_l = load_list("cand_l", cand)
-        w2_raw.append(load_weight("w2", w2, 384, 512))
+        w2_raw.append(load_weight("w2", w2, *W2_PIECES[2]))
         nc.sync.dma_start(table_words[:].bitcast(I32), x_words[0].rearrange("p c r -> p (c r)").bitcast(I32))
-        w1_raw = [load_weight("w1", w1, lo, hi) for lo, hi in ((0, 128), (128, 256), (256, 512))]
+        w1_raw = [load_weight("w1", w1, lo, hi) for lo, hi in W1_PIECES]
         n2_l = load_list("n2_l", n2)
         gs_sb = sb("gs_sb", [P, PACK], F32)
         nc.sync.dma_start(gs_sb[:], gs.rearrange("(p t) o -> p (t o)", t=PACK))
@@ -84,8 +103,10 @@ def tile_picked_twcpullbhopp_none_p_kernel(tc, x_words, x_scales, w1, w2, gs, of
 
         def round_weight(grouped, piece):
             raw, lo, hi = piece
-            dst = grouped[:].rearrange("p (t m j) -> p m j t", t=PACK, j=PACK)[:, lo // PACK : hi // PACK]
-            nc.scalar.copy(dst, raw[:].rearrange("p j (m t) -> p m j t", t=PACK))
+            dst = grouped[:].rearrange("p (a e m j) -> p a m j e", e=PAIR, m=P, j=PACK)
+            src = raw[:].rearrange("p j (m a e) -> p a m j e", a=PACK // PAIR, e=PAIR)
+            for a in range(PACK // PAIR):
+                nc.scalar.copy(dst[:, a, lo // PACK : hi // PACK], src[:, a])
 
         def quantize(name, src, width):
             codes = sb(name + "_codes", [P, width], U32)
@@ -110,7 +131,7 @@ def tile_picked_twcpullbhopp_none_p_kernel(tc, x_words, x_scales, w1, w2, gs, of
             round_weight(w2_grouped, piece)
         w2_q = quantize("w2", w2_grouped[:], H)
         two_words = gather_words("two_words", two_l)
-        d_ps = [psum.tile([P, S], F32, name="d_ps%d" % t, tag="bank%d" % t) for t in range(PACK)]
+        d_ps = [bank_tile("d_ps%d" % t, S, t) for t in range(PACK)]
         for t in range(PACK):
             product(d_ps[t][:], w2_q, t, (two_words, two_scales))
         offs_words = gather_words("offs_words", offs_l)
@@ -121,6 +142,7 @@ def tile_picked_twcpullbhopp_none_p_kernel(tc, x_words, x_scales, w1, w2, gs, of
             cand_scales[:].bitcast(I32).rearrange("p (t q) -> p t q", t=PACK),
             cand_scales_listed[:].bitcast(I32).rearrange("p (q t) -> p t q", t=PACK),
         )
+        cand_q = (cand_words, cand_scales)
 
         def d_out(t):
             nc.scalar.copy(d_win[t][:, :S], d_ps[t][:])
@@ -137,39 +159,35 @@ def tile_picked_twcpullbhopp_none_p_kernel(tc, x_words, x_scales, w1, w2, gs, of
         d_diff(0)
         w1_q = quantize("w1", w1_grouped[:], H)
         d_diff(1)
-        y_ps = [psum.tile([P, S], F32, name="y_ps%d" % t, tag="bank%d" % (PACK + t)) for t in range(PACK)]
+        y_ps = [bank_tile("y_ps%d" % t, S, PACK + t) for t in range(PACK)]
         for t in range(PACK):
             product(y_ps[t][:], w1_q, t, (offs_words, offs_scales))
         for t in range(2, PACK):
             d_out(t)
             d_diff(t)
 
-        HALF = S // 2
-        QUARTER = S // 4
         stayed = sb("stayed", [P, PACK, S], F32)
         pulled_early = sb("pulled_early", [P, PACK, HALF], F32)
 
         def pull(dst, t, lo, hi):
-            nc.vector.tensor_tensor(dst, y_win[t][:].indirect(n1_l[:, lo // 16 : hi // 16]), st_win[t][:, S + lo : S + hi], ALU.mult)
+            nc.vector.tensor_tensor(dst, y_win[t][:].indirect(entries(n1_l, lo, hi)), gate[t][:, lo:hi], ALU.mult)
 
         def blend(z_grouped, pulled, lo, hi):
             nc.vector.tensor_tensor(
-                z_grouped.rearrange("p (c i t) -> p c t i", i=PACK, t=PACK),
-                pulled.rearrange("p t (c i) -> p c t i", i=PACK),
-                stayed[:, :, lo:hi].rearrange("p t (c i) -> p c t i", i=PACK),
+                z_grouped.rearrange("p (c i t) -> p c t i", i=PAIR, t=PACK),
+                pulled.rearrange("p t (c i) -> p c t i", i=PAIR),
+                stayed[:, :, lo:hi].rearrange("p t (c i) -> p c t i", i=PAIR),
                 ALU.subtract,
             )
 
         def s_out(t, lo, hi, bank):
-            nc.scalar.activation(s_win[t][:, lo:hi], bank, ACT.Copy, scale=0.125)
-            nc.scalar.activation(s_twin[t][:, lo:hi], bank, ACT.Copy, scale=0.125)
+            nc.scalar.activation(s_win[t][:, lo:hi], bank, ACT.Copy, scale=S_SCALE)
+            nc.scalar.activation(s_twin[t][:, lo:hi], bank, ACT.Copy, scale=S_SCALE)
 
-        cand_q = (cand_words, cand_scales)
         for t in range(PACK):
-            gate = st_win[t][:, S:]
             nc.scalar.activation(y_win[t][:, :S], y_ps[t][:], ACT.Copy, scale=gs_sb[:, t : t + 1])
-            nc.scalar.activation(gate, diff[t], ACT.Sigmoid)
-            nc.vector.scalar_tensor_tensor(stayed[:, t, :], gate, 1.0, y_win[t][:, :S], ALU.subtract, ALU.mult)
+            nc.scalar.activation(gate[t], diff[t], ACT.Sigmoid)
+            nc.vector.scalar_tensor_tensor(stayed[:, t, :], gate[t], 1.0, y_win[t][:, :S], ALU.subtract, ALU.mult)
             pull(pulled_early[:, t, :], t, 0, HALF)
 
         pulled_late = keep.tile([P, PACK, HALF], F32, name="pulled_late", tag="late", align_bytes=64)
@@ -179,54 +197,56 @@ def tile_picked_twcpullbhopp_none_p_kernel(tc, x_words, x_scales, w1, w2, gs, of
         pull(pulled_late[:, 1, :], 1, HALF, S)
         z_early_q = quantize("z_early", z_early[:], HALF)
         for t in range(PACK):
-            bank = psum.tile([P, HALF], F32, name="s_early%d" % t, tag="bank%d" % t)
+            bank = bank_tile("s_early%d" % t, HALF, t)
             product(bank[:], cand_q, t, z_early_q)
             s_out(t, 0, HALF, bank[:])
         pull(pulled_late[:, 2, :], 2, HALF, S)
-        for lo in (0, QUARTER):
-            pull(pulled_late[:, 3, lo : lo + QUARTER], 3, HALF + lo, HALF + lo + QUARTER)
+
+        quarters = (0, QUARTER)
+        for lo in quarters:
+            pull(pulled_late[:, LAST, lo : lo + QUARTER], LAST, HALF + lo, HALF + lo + QUARTER)
         z_late = sb("z_late", [P, PACK * HALF], BF16)
         z_late_codes = sb("z_late_codes", [P, HALF], U32)
         z_late_scales = sb("z_late_scales", [P, HALF], U8)
-        for lo in (0, QUARTER):
+        for lo in quarters:
             blend(z_late[:, PACK * lo : PACK * (lo + QUARTER)], pulled_late[:, :, lo : lo + QUARTER], HALF + lo, HALF + lo + QUARTER)
-        for i, lo in enumerate((0, QUARTER)):
+
+        def score_quarter(name, lo, bank_no):
             cols = slice(lo, lo + QUARTER)
-            nc.vector.quantize_mx(out=z_late_codes[:, cols].bitcast(FP8X4), scales=z_late_scales[:, cols], in_=z_late[:, PACK * lo : PACK * (lo + QUARTER)])
-            bank = psum.tile([P, QUARTER], F32, name="s_first%d" % i, tag="bank%d" % (PACK * i))
+            nc.vector.quantize_mx(
+                out=z_late_codes[:, cols].bitcast(FP8X4), scales=z_late_scales[:, cols], in_=z_late[:, PACK * lo : PACK * (lo + QUARTER)]
+            )
+            bank = bank_tile(name, QUARTER, bank_no)
             product(bank[:], cand_q, 0, (z_late_codes[:, cols], z_late_scales[:, cols]))
-            if i == 0:
-                s_out(0, HALF + lo, HALF + lo + QUARTER, bank[:])
-            else:
-                nc.vector.tensor_scalar(s_win[0][:, HALF + lo : S], bank[:], 0.125, None, ALU.mult)
-                nc.scalar.activation(s_twin[0][:, HALF + lo : S], bank[:], ACT.Copy, scale=0.125)
-        late = {}
+            return bank
+
+        s_out(0, HALF, HALF + QUARTER, score_quarter("s_first0", 0, 0)[:])
+        bank = score_quarter("s_first1", QUARTER, PACK)
+        nc.vector.tensor_scalar(s_win[0][:, HALF + QUARTER : S], bank[:], S_SCALE, None, ALU.mult)
+        nc.scalar.activation(s_twin[0][:, HALF + QUARTER : S], bank[:], ACT.Copy, scale=S_SCALE)
+        s_late = {}
         for t in range(1, PACK):
-            late[t] = psum.tile([P, HALF], F32, name="s_late%d" % t, tag="bank%d" % (PACK + t))
-            product(late[t][:], cand_q, t, (z_late_codes, z_late_scales))
+            s_late[t] = bank_tile("s_late%d" % t, HALF, PACK + t)
+            product(s_late[t][:], cand_q, t, (z_late_codes, z_late_scales))
 
         rows = out.rearrange("(q t u) n -> t q u n", t=PACK, u=PACK)
         squash = [sb("squash%d" % t, [P, S], F32) for t in range(PACK)]
         result = [sb("result%d" % t, [P, S], F32) for t in range(PACK)]
 
-        def pair_up(t, lo=0, hi=S):
-            nc.vector.tensor_tensor(st_win[t][:, lo:hi], s_win[t][:].indirect(n3_l[:, lo // 16 : hi // 16]), s_twin[t][:, lo:hi], ALU.add)
-
-        def look_up(t, lo, hi):
-            nc.scalar.activation(squash[t][:, lo:hi], st_win[t][:].indirect(n4_l[:, lo // 16 : hi // 16]), ACT.Sigmoid)
+        def pair_up(t, lo, hi):
+            nc.vector.tensor_tensor(st_win[t][:, lo:hi], s_win[t][:].indirect(entries(n3_l, lo, hi)), s_twin[t][:, lo:hi], ALU.add)
 
         def finish(t, lo, hi):
+            nc.scalar.activation(squash[t][:, lo:hi], st_win[t][:].indirect(entries(n4_l, lo, hi)), ACT.Sigmoid)
             nc.vector.scalar_tensor_tensor(result[t][:, lo:hi], squash[t][:, lo:hi], 0.5, st_win[t][:, lo:hi], ALU.subtract, ALU.mult)
             nc.sync.dma_start(rows[t][:, :, lo:hi], result[t][:, lo:hi])
 
         pair_up(0, 0, HALF)
         pair_up(0, HALF, S)
         for t in range(1, PACK):
-            s_out(t, HALF, S, late[t][:])
-            pair_up(t)
-        for t in range(PACK - 1):
-            look_up(t, 0, S)
+            s_out(t, HALF, S, s_late[t][:])
+            pair_up(t, 0, S)
+        for t in range(LAST):
             finish(t, 0, S)
-        for lo, hi in ((0, HALF), (HALF, S)):
-            look_up(PACK - 1, lo, hi)
-            finish(PACK - 1, lo, hi)
+        finish(LAST, 0, HALF)
+        finish(LAST, HALF, S)

from contextlib import ExitStack

import concourse.mybir as mybir

K, T, S, H, C = 512, 2048, 512, 512, 512
FLOPS = 2 * K * (2 * H * S + C * S)

F32 = mybir.dt.float32
BF16 = mybir.dt.bfloat16
I32 = mybir.dt.int32
U32 = mybir.dt.uint32
U16 = mybir.dt.uint16
U8 = mybir.dt.uint8
FP8X4 = mybir.dt.float8_e4m3fn_x4
ALU = mybir.AluOpType
ACT = mybir.ActivationFunctionType

P = 128
PACK = 4
LAST = PACK - 1
STRIPE = 16
QUADRANT = 32
SCALE_ROWS = 4
HALF = S // 2
QUARTER = S // 4
S_SCALE = 2 * 0.0625
PAIR = 2

W2_PIECES = ((0, 128), (128, 384), (384, 512))
W1_PIECES = ((0, 128), (128, 256), (256, 512))


def tile_picked_twcpullbhopp_none_p_kernel(
    tc, x_words, x_scales, w1, w2, gs, offs, two, n1, n2, cand, n3, n4, out
):
    nc = tc.nc
    with ExitStack() as ctx:
        keep = ctx.enter_context(tc.tile_pool(name="keep", bufs=1))
        psum = ctx.enter_context(tc.psum_pool(name="psum", bufs=1))

        def sb(name, shape, dtype):
            return keep.tile(shape, dtype, name=name, align_bytes=64)

        def bank_tile(name, width, bank_no):
            return psum.tile([P, width], F32, name=name, tag="bank%d" % bank_no)

        def load_list(name, src):
            tile = keep.tile([P, S // STRIPE], U16, name=name)
            nc.sync.dma_start(tile[:], src)
            return tile

        def entries(lst, lo, hi):
            return lst[:, lo // STRIPE : hi // STRIPE]

        def load_weight(name, w, lo, hi):
            tile = sb("%s_raw%d" % (name, lo), [P, PACK, hi - lo], F32)
            nc.sync.dma_start(tile[:], w.rearrange("(p j) c -> p j c", j=PACK)[:, :, lo:hi])
            return tile, lo, hi

        table_scales = sb("table_scales", [P, T], U8)
        table_words = sb("table_words", [P, T], U32)
        d_win = [sb("d_win%d" % t, [P, 2 * S], F32) for t in range(PACK)]
        y_win = [sb("y_win%d" % t, [P, 2 * S], F32) for t in range(PACK)]
        s_win = [sb("s_win%d" % t, [P, 2 * S], F32) for t in range(PACK)]
        st_win = [sb("st_win%d" % t, [P, 2 * S], F32) for t in range(PACK)]
        s_last = sb("s_last", [P, S], F32)
        last_diff = keep.tile([P, S], F32, name="last_diff", tag="late", align_bytes=64)
        d_twin = [d_win[t + 1][:, S:] for t in range(LAST)] + [y_win[LAST][:, S:]]
        s_twin = [s_win[t + 1][:, S:] for t in range(LAST)] + [s_last[:]]
        diff = [y_win[t][:, S:] for t in range(LAST)] + [last_diff[:]]
        gate = [st_win[t][:, S:] for t in range(PACK)]

        nc.vector.memset(table_scales[:].bitcast(I32), 0)
        w2_raw = [load_weight("w2", w2, *W2_PIECES[0])]
        two_l = load_list("two_l", two)
        offs_l = load_list("offs_l", offs)
        for r in range(SCALE_ROWS):
            nc.sync.dma_start(table_scales[r:P:QUADRANT, :].bitcast(I32), x_scales[0, r : K // 32 : SCALE_ROWS, :].bitcast(I32))
        w2_raw.append(load_weight("w2", w2, *W2_PIECES[1]))
        cand_l = load_list("cand_l", cand)
        w2_raw.append(load_weight("w2", w2, *W2_PIECES[2]))
        nc.sync.dma_start(table_words[:].bitcast(I32), x_words[0].rearrange("p c r -> p (c r)").bitcast(I32))
        w1_raw = [load_weight("w1", w1, lo, hi) for lo, hi in W1_PIECES]
        n2_l = load_list("n2_l", n2)
        gs_sb = sb("gs_sb", [P, PACK], F32)
        nc.sync.dma_start(gs_sb[:], gs.rearrange("(p t) o -> p (t o)", t=PACK))
        n1_l = load_list("n1_l", n1)
        n3_l = load_list("n3_l", n3)
        n4_l = load_list("n4_l", n4)

        nc.vector.memset(d_win[0][:, S:], 0.0)
        nc.scalar.activation(s_win[0][:, S:], d_win[0][:, S:], ACT.Sigmoid)

        def gather_scales(name, lst):
            tile = sb(name, [P, S], U8)
            nc.vector.tensor_copy(tile[:], table_scales[:].indirect(lst[:]))
            return tile

        def gather_words(name, lst):
            tile = sb(name, [P, S], U32)
            nc.vector.tensor_copy(tile[:], table_words[:].indirect(lst[:]))
            return tile

        def round_weight(grouped, piece):
            raw, lo, hi = piece
            dst = grouped[:].rearrange("p (a e m j) -> p a m j e", e=PAIR, m=P, j=PACK)
            src = raw[:].rearrange("p j (m a e) -> p a m j e", a=PACK // PAIR, e=PAIR)
            for a in range(PACK // PAIR):
                nc.scalar.copy(dst[:, a, lo // PACK : hi // PACK], src[:, a])

        def quantize(name, src, width):
            codes = sb(name + "_codes", [P, width], U32)
            scales = sb(name + "_scales", [P, width], U8)
            nc.vector.quantize_mx(out=codes[:].bitcast(FP8X4), scales=scales[:], in_=src)
            return codes, scales

        def product(dst, lhs, t, rhs):
            cols = slice(t * P, (t + 1) * P)
            nc.tensor.matmul_mx(
                out=dst, lhsT=lhs[0][:, cols].bitcast(FP8X4), lhsT_scale=lhs[1][:, cols],
                rhs=rhs[0][:].bitcast(FP8X4), rhs_scale=rhs[1][:], start=True, stop=True,
            )

        w2_grouped = sb("w2_grouped", [P, PACK * H], BF16)
        w1_grouped = sb("w1_grouped", [P, PACK * H], BF16)

        two_scales = gather_scales("two_scales", two_l)
        offs_scales = gather_scales("offs_scales", offs_l)
        cand_scales_listed = gather_scales("cand_scales_listed", cand_l)
        for piece in w2_raw:
            round_weight(w2_grouped, piece)
        w2_q = quantize("w2", w2_grouped[:], H)
        two_words = gather_words("two_words", two_l)
        d_ps = [bank_tile("d_ps%d" % t, S, t) for t in range(PACK)]
        for t in range(PACK):
            product(d_ps[t][:], w2_q, t, (two_words, two_scales))
        offs_words = gather_words("offs_words", offs_l)
        cand_words = sb("cand_words", [P, C], U32)
        nc.vector.tensor_copy(cand_words[:].rearrange("p (t q u) -> p q t u", t=PACK, u=PACK), table_words[:].indirect(cand_l[:]))
        cand_scales = sb("cand_scales", [P, C], U8)
        nc.vector.tensor_copy(
            cand_scales[:].bitcast(I32).rearrange("p (t q) -> p t q", t=PACK),
            cand_scales_listed[:].bitcast(I32).rearrange("p (q t) -> p t q", t=PACK),
        )
        cand_q = (cand_words, cand_scales)

        def d_out(t):
            nc.scalar.copy(d_win[t][:, :S], d_ps[t][:])
            nc.scalar.copy(d_twin[t], d_ps[t][:])

        def d_diff(t):
            nc.vector.tensor_tensor(diff[t], d_win[t][:].indirect(n2_l[:]), d_twin[t], ALU.subtract)

        round_weight(w1_grouped, w1_raw[0])
        round_weight(w1_grouped, w1_raw[1])
        d_out(0)
        round_weight(w1_grouped, w1_raw[2])
        d_out(1)
        d_diff(0)
        w1_q = quantize("w1", w1_grouped[:], H)
        d_diff(1)
        y_ps = [bank_tile("y_ps%d" % t, S, PACK + t) for t in range(PACK)]
        for t in range(PACK):
            product(y_ps[t][:], w1_q, t, (offs_words, offs_scales))
        for t in range(2, PACK):
            d_out(t)
            d_diff(t)

        stayed = sb("stayed", [P, PACK, S], F32)
        pulled_early = sb("pulled_early", [P, PACK, HALF], F32)

        def pull(dst, t, lo, hi):
            nc.vector.tensor_tensor(dst, y_win[t][:].indirect(entries(n1_l, lo, hi)), gate[t][:, lo:hi], ALU.mult)

        def blend(z_grouped, pulled, lo, hi):
            nc.vector.tensor_tensor(
                z_grouped.rearrange("p (c i t) -> p c t i", i=PAIR, t=PACK),
                pulled.rearrange("p t (c i) -> p c t i", i=PAIR),
                stayed[:, :, lo:hi].rearrange("p t (c i) -> p c t i", i=PAIR),
                ALU.subtract,
            )

        def s_out(t, lo, hi, bank):
            nc.scalar.activation(s_win[t][:, lo:hi], bank, ACT.Copy, scale=S_SCALE)
            nc.scalar.activation(s_twin[t][:, lo:hi], bank, ACT.Copy, scale=S_SCALE)

        for t in range(PACK):
            nc.scalar.activation(y_win[t][:, :S], y_ps[t][:], ACT.Copy, scale=gs_sb[:, t : t + 1])
            nc.scalar.activation(gate[t], diff[t], ACT.Sigmoid)
            nc.vector.scalar_tensor_tensor(stayed[:, t, :], gate[t], 1.0, y_win[t][:, :S], ALU.subtract, ALU.mult)
            pull(pulled_early[:, t, :], t, 0, HALF)

        pulled_late = keep.tile([P, PACK, HALF], F32, name="pulled_late", tag="late", align_bytes=64)
        z_early = sb("z_early", [P, PACK * HALF], BF16)
        pull(pulled_late[:, 0, :], 0, HALF, S)
        blend(z_early[:], pulled_early[:], 0, HALF)
        pull(pulled_late[:, 1, :], 1, HALF, S)
        z_early_q = quantize("z_early", z_early[:], HALF)
        for t in range(PACK):
            bank = bank_tile("s_early%d" % t, HALF, t)
            product(bank[:], cand_q, t, z_early_q)
            s_out(t, 0, HALF, bank[:])
        pull(pulled_late[:, 2, :], 2, HALF, S)

        quarters = (0, QUARTER)
        for lo in quarters:
            pull(pulled_late[:, LAST, lo : lo + QUARTER], LAST, HALF + lo, HALF + lo + QUARTER)
        z_late = sb("z_late", [P, PACK * HALF], BF16)
        z_late_codes = sb("z_late_codes", [P, HALF], U32)
        z_late_scales = sb("z_late_scales", [P, HALF], U8)
        for lo in quarters:
            blend(z_late[:, PACK * lo : PACK * (lo + QUARTER)], pulled_late[:, :, lo : lo + QUARTER], HALF + lo, HALF + lo + QUARTER)

        def score_quarter(name, lo, bank_no):
            cols = slice(lo, lo + QUARTER)
            nc.vector.quantize_mx(
                out=z_late_codes[:, cols].bitcast(FP8X4), scales=z_late_scales[:, cols], in_=z_late[:, PACK * lo : PACK * (lo + QUARTER)]
            )
            bank = bank_tile(name, QUARTER, bank_no)
            product(bank[:], cand_q, 0, (z_late_codes[:, cols], z_late_scales[:, cols]))
            return bank

        s_out(0, HALF, HALF + QUARTER, score_quarter("s_first0", 0, 0)[:])
        bank = score_quarter("s_first1", QUARTER, PACK)
        nc.vector.tensor_scalar(s_win[0][:, HALF + QUARTER : S], bank[:], S_SCALE, None, ALU.mult)
        nc.scalar.activation(s_twin[0][:, HALF + QUARTER : S], bank[:], ACT.Copy, scale=S_SCALE)
        s_late = {}
        for t in range(1, PACK):
            s_late[t] = bank_tile("s_late%d" % t, HALF, PACK + t)
            product(s_late[t][:], cand_q, t, (z_late_codes, z_late_scales))

        rows = out.rearrange("(q t u) n -> t q u n", t=PACK, u=PACK)
        squash = [sb("squash%d" % t, [P, S], F32) for t in range(PACK)]
        result = [sb("result%d" % t, [P, S], F32) for t in range(PACK)]

        def pair_up(t, lo, hi):
            nc.vector.tensor_tensor(st_win[t][:, lo:hi], s_win[t][:].indirect(entries(n3_l, lo, hi)), s_twin[t][:, lo:hi], ALU.add)

        def finish(t, lo, hi):
            nc.scalar.activation(squash[t][:, lo:hi], st_win[t][:].indirect(entries(n4_l, lo, hi)), ACT.Sigmoid)
            nc.vector.scalar_tensor_tensor(result[t][:, lo:hi], squash[t][:, lo:hi], 0.5, st_win[t][:, lo:hi], ALU.subtract, ALU.mult)
            nc.sync.dma_start(rows[t][:, :, lo:hi], result[t][:, lo:hi])

        pair_up(0, 0, HALF)
        pair_up(0, HALF, S)
        for t in range(1, PACK):
            s_out(t, HALF, S, s_late[t][:])
            pair_up(t, 0, S)
        for t in range(LAST):
            finish(t, 0, S)
        finish(LAST, 0, HALF)
        finish(LAST, HALF, S)
